import numpy as np
import ml_dtypes


def mxq(x, axis, fmt="e4m3"):
    dtype, down = {"e4m3": (ml_dtypes.float8_e4m3fn, 7), "e5m2": (ml_dtypes.float8_e5m2, 14)}[fmt]
    v = np.moveaxis(np.asarray(x, np.float32).astype(ml_dtypes.bfloat16).astype(np.float64), axis, -1)
    blocks = v.reshape(v.shape[:-1] + (-1, 32))
    amax = np.abs(blocks).max(-1, keepdims=True)
    byte = np.maximum(np.where(amax > 0, np.frexp(amax)[1] - 1 + 127, 0) - down, 1)
    scale = np.exp2(byte - 127.0)
    codes = (blocks / scale).astype(np.float32).astype(dtype).astype(np.float64)
    return np.moveaxis((codes * scale).reshape(v.shape), -1, axis)


WIDE = False


def mx_kscale(k):
    if not WIDE:
        return np.ones(k)
    levels = np.array([10, -10, 5, -5, 0])
    if k % 512:
        return np.exp2(np.random.permutation(np.resize(levels, k // 32))).repeat(32)
    a = np.empty((k // 512, 16))
    for p in range(k // 512):
        a[p, :8] = np.random.permutation(np.resize(levels, 8))
        for g in range(8):
            far = levels[np.abs(levels - a[p, g]) >= 10]
            a[p, g + 8] = far[np.random.randint(len(far))]
    return np.exp2(a.ravel()).repeat(32)


BF16 = ml_dtypes.bfloat16


def bf(x):
    return np.asarray(x, np.float32).astype(BF16)


def f64(x):
    return np.asarray(x).astype(np.float64)

E4M3FN = np.array([(-1.0 if i & 128 else 1.0) * ((1.0 + (i & 7) / 8.0) * 2.0 ** (((i >> 3) & 15) - 7) if i & 120 else (i & 7) * 2.0 ** -9) for i in range(256)])


def e4m3fn_bytes(y):
    return np.clip(np.asarray(y, np.float64), -448.0, 448.0).astype(np.float32).astype(ml_dtypes.float8_e4m3fn).view(np.uint8)


def e4m3fn_values(b):
    return E4M3FN[b]


P, C, H, Q = 1024, 512, 2048, 128


def setup_inputs():
    s, t = mx_kscale(C), mx_kscale(H)
    w1 = np.random.standard_normal((C, H)) / np.sqrt(C) / s[:, None]
    w2 = np.random.standard_normal((C, H)) / np.sqrt(H) / t
    w1_scale = (np.abs(w1).reshape(C // Q, Q, H // Q, Q).max(axis=(1, 3)) / 448.0).astype(np.float32)
    w2_scale = (np.abs(w2).reshape(C // Q, Q, H // Q, Q).max(axis=(1, 3)) / 448.0).astype(np.float32)
    return {"y": bf(np.random.standard_normal((P, C)) * s),
            "w1_bytes": e4m3fn_bytes(w1 / np.repeat(np.repeat(f64(w1_scale), Q, axis=0), Q, axis=1)),
            "w1_scale": w1_scale,
            "g": bf((1 + 0.1 * np.random.standard_normal(H)) * t),
            "w2_bytes": e4m3fn_bytes(w2 / np.repeat(np.repeat(f64(w2_scale), Q, axis=0), Q, axis=1)),
            "w2_scale": w2_scale,
            "gamma": bf(1 + 0.1 * np.random.standard_normal(C)),
            "r": bf(np.random.standard_normal((C, P)))}


def reference(y, w1_bytes, w1_scale, g, w2_bytes, w2_scale, gamma, r):
    w1 = e4m3fn_values(w1_bytes) * np.repeat(np.repeat(f64(w1_scale), Q, axis=0), Q, axis=1)
    w2 = e4m3fn_values(w2_bytes) * np.repeat(np.repeat(f64(w2_scale), Q, axis=0), Q, axis=1)
    z = mxq(f64(y), 1, "e4m3") @ mxq(w1, 0, "e4m3")
    a = 0.5 * z * (1 + np.tanh(np.sqrt(2 / np.pi) * (z + 0.044715 * z * z * z)))
    h = a * f64(g)
    o = mxq(w2, 1, "e4m3") @ mxq(h, 1, "e4m3").T
    return f64(r) + f64(gamma)[:, None] * o

@@ -1,0 +1,291 @@
+from contextlib import ExitStack
+
+import concourse.mybir as mybir
+from concourse.masks import make_identity
+
+F32 = mybir.dt.float32
+BF16 = mybir.dt.bfloat16
+U32 = mybir.dt.uint32
+U8 = mybir.dt.uint8
+FP8 = mybir.dt.float8_e4m3fn
+FP8X4 = mybir.dt.float8_e4m3fn_x4
+MULT = mybir.AluOpType.mult
+ADD = mybir.AluOpType.add
+GELU = mybir.ActivationFunctionType.Gelu_apprx_tanh
+COPY = mybir.ActivationFunctionType.Copy
+
+P = 128
+NPOS, C, H = 1024, 512, 2048
+NG = H // 512
+NI = C // P
+FLOPS = 2 * NPOS * C * H * 2
+
+S_EXIT = [(1, k) for k in range(4)]
+
+
+def tile_convnext_pointwise_pair_d7_kernel(
+    tc, y, w1_bytes, w1_scale, g, w2_bytes, w2_scale, gamma, r, out
+):
+    nc = tc.nc
+    with ExitStack() as ctx:
+        keep = ctx.enter_context(tc.tile_pool(name="keep", bufs=1))
+        gelp = ctx.enter_context(tc.tile_pool(name="gelp", bufs=12))
+        hp = ctx.enter_context(tc.tile_pool(name="hp", bufs=3))
+        op = ctx.enter_context(tc.tile_pool(name="op", bufs=1))
+        psum = ctx.enter_context(tc.psum_pool(name="psum", bufs=1))
+        ctx.enter_context(tc.manual_schedule())
+
+        def sb(shape, dt, name):
+            return keep.tile(shape, dt, name=name, align_bytes=64)
+
+        ident = sb([P, P], F32, "ident")
+        w1s = sb([P, 16], F32, "w1s")
+        w2s_all = sb([P, 4, 16], F32, "w2s_all")
+        w2s = sb([P, 4, 4], F32, "w2s")
+        g_sb = sb([P, 16], BF16, "g_sb")
+        gamma_sb = sb([P, 4, 2], BF16, "gamma_sb")
+        y_sb = [sb([P, 2, C], BF16, "y_sb%d" % p) for p in range(4)]
+        y_grp = [sb([P, 1024], BF16, "y_grp%d" % p) for p in range(4)]
+        y_codes = sb([P, NPOS], U32, "y_codes")
+        y_scl = sb([P, NPOS], U8, "y_scl")
+        w1_raw = [sb([P, 2048], U8, "w1_raw%d" % k) for k in range(NG)]
+        w1_wide = [sb([P, 2048], BF16, "w1_wide%d" % k) for k in range(NG)]
+        w1_grp = [sb([P, 2048], BF16, "w1_grp%d" % k) for k in range(NG)]
+        w1_codes = [sb([P, 512], U32, "w1_codes%d" % k) for k in range(NG)]
+        w1_scl = [sb([P, 512], U8, "w1_scl%d" % k) for k in range(NG)]
+        w2_raw = [sb([P, 2048], U8, "w2_raw%d" % i) for i in range(NI)]
+        w2_wide = [sb([P, 2048], BF16, "w2_wide%d" % i) for i in range(NI)]
+        w2_grp = [sb([P, 2048], BF16, "w2_grp%d" % k) for k in range(NG)]
+        w2_codes = [sb([P, 512], U32, "w2_codes%d" % k) for k in range(NG)]
+        w2_scl = [sb([P, 512], U8, "w2_scl%d" % k) for k in range(NG)]
+        h_codes = [[sb([P, 512], U32, "h_codes%d_%d" % (k, n)) for n in range(2)] for k in range(NG)]
+        h_scl = [[sb([P, 512], U8, "h_scl%d_%d" % (k, n)) for n in range(2)] for k in range(NG)]
+        r_sb = sb([P, NI, NPOS], BF16, "r_sb")
+
+        gel = {}
+        hbf = {}
+        acc = {}
+        tb = {}
+
+        def load_w1(k):
+            src = w1_bytes.rearrange("(p t) n -> p t n", t=4)[:, :, 512 * k : 512 * (k + 1)]
+            nc.sync.dma_start(out=w1_raw[k][:].rearrange("p (t n) -> p t n", t=4), in_=src)
+
+        def load_y(p):
+            nc.sync.dma_start(
+                out=y_sb[p][:], in_=y[256 * p : 256 * (p + 1), :].rearrange("(a p) k -> p a k", p=P)
+            )
+
+        def load_w2(i):
+            nc.sync.dma_start(out=w2_raw[i][:], in_=w2_bytes[P * i : P * (i + 1), :])
+
+        def widen(eng, dst, src, lo, hi):
+            d, s = dst[:, lo:hi], src[:, lo:hi].bitcast(FP8)
+            if eng == "s":
+                nc.scalar.copy(out=d, in_=s)
+            else:
+                nc.vector.tensor_copy(out=d, in_=s)
+
+        def interleave_w1(k, jb):
+            o = w1_grp[k][:].rearrange("p (t m j) -> p m j t", t=4, j=4)[:, 32 * jb : 32 * (jb + 1)]
+            i = w1_wide[k][:].rearrange("p (j m t) -> p m j t", j=4, t=4)[:, 32 * jb : 32 * (jb + 1)]
+            nc.vector.tensor_scalar(
+                out=o, in0=i, scalar1=w1s[:, 4 * k + jb : 4 * k + jb + 1], scalar2=None, op0=MULT
+            )
+
+        def quant_w1(k):
+            nc.vector.quantize_mx(out=w1_codes[k][:].bitcast(FP8X4), scales=w1_scl[k][:], in_=w1_grp[k][:])
+
+        def turn_y(p):
+            t = psum.tile([P, 2, 2, P], F32, name="a%d" % p)
+            words = y_sb[p][:].rearrange("p a k -> p (a k)").bitcast(F32)
+            for a in range(2):
+                for u in range(2):
+                    nc.tensor.transpose(t[:, a, u, :], words[:, 256 * a + u : 256 * (a + 1) : 2], ident[:])
+            return t
+
+        def exit_y(eng, p, t):
+            o = y_grp[p][:].bitcast(F32).rearrange("p (a r u) -> p a r u", a=2, u=2)
+            i = t[:].rearrange("p a u r -> p a r u")
+            if eng == "s":
+                nc.scalar.copy(out=o, in_=i)
+            else:
+                nc.vector.tensor_copy(out=o, in_=i)
+
+        def quant_y(p):
+            cols = slice(256 * p, 256 * (p + 1))
+            nc.vector.quantize_mx(out=y_codes[:, cols].bitcast(FP8X4), scales=y_scl[:, cols], in_=y_grp[p][:])
+
+        def z_unit(u):
+            k, b = divmod(u, 8)
+            z = psum.tile([P, 4, P], F32, name="z%d" % (u % 4))
+            for t in range(4):
+                nc.tensor.matmul_mx(
+                    out=z[:, t, :],
+                    lhsT=w1_codes[k][:, P * t : P * (t + 1)].bitcast(FP8X4),
+                    lhsT_scale=w1_scl[k][:, P * t : P * (t + 1)],
+                    rhs=y_codes[:, P * b : P * (b + 1)].bitcast(FP8X4),
+                    rhs_scale=y_scl[:, P * b : P * (b + 1)],
+                    start=True,
+                    stop=True,
+                )
+            return z
+
+        def gelu(u, z):
+            a = gelp.tile([P, P, 4], F32, name="gel")
+            nc.scalar.activation(out=a[:], in_=z[:].rearrange("p t n -> p n t"), func=GELU)
+            gel[u] = a
+
+        def gain(u):
+            k = u // 8
+            if u % 2 == 0:
+                hb = hp.tile([P, 1024], BF16, name="hbf", align_bytes=64)
+                hbf[u // 2] = hb
+            o = hbf[u // 2][:, 512 * (u % 2) : 512 * (u % 2 + 1)].rearrange("p (n t) -> p n t", t=4)
+            gk = g_sb[:, 4 * k : 4 * (k + 1)].unsqueeze(1).to_broadcast([P, P, 4])
+            nc.vector.tensor_tensor(out=o, in0=gel[u][:], in1=gk, op=MULT)
+
+        def quant_h(pair):
+            k, q = divmod(pair, 4)
+            n, c = divmod(q, 2)
+            cols = slice(256 * c, 256 * (c + 1))
+            nc.vector.quantize_mx(
+                out=h_codes[k][n][:, cols].bitcast(FP8X4), scales=h_scl[k][n][:, cols], in_=hbf[pair][:]
+            )
+
+        def turn_w2(ip, k, bank):
+            t = psum.tile([P, 2, 2, P], F32, name="a%d" % bank)
+            for ii in range(2):
+                words = w2_wide[2 * ip + ii][:].bitcast(F32)
+                for u in range(2):
+                    nc.tensor.transpose(t[:, ii, u, :], words[:, 256 * k + u : 256 * (k + 1) : 2], ident[:])
+            tb[ip, k] = t
+
+        def exit_w2(i, k):
+            o = w2_grp[k][:, 512 * i : 512 * (i + 1)].rearrange("p (r u e) -> p r u e", u=2, e=2)
+            s = tb[i // 2, k][:, i % 2].rearrange("p u r -> p (u r)").bitcast(BF16)
+            s = s.rearrange("p (u r e) -> p r u e", u=2, e=2)
+            col = w2s[:, i, k : k + 1]
+            if (i // 2, k) in S_EXIT:
+                nc.scalar.activation(out=o, in_=s, func=COPY, scale=col)
+            else:
+                nc.vector.tensor_scalar(out=o, in0=s, scalar1=col, scalar2=None, op0=MULT)
+
+        def quant_w2(k):
+            nc.vector.quantize_mx(out=w2_codes[k][:].bitcast(FP8X4), scales=w2_scl[k][:], in_=w2_grp[k][:])
+
+        def stage2(n, i, k):
+            if k == 0:
+                acc[n, i] = psum.tile([P, 512], F32, name="z0" if (n, i) == (1, 3) else "a%d" % i)
+            nc.tensor.matmul_mx(
+                out=acc[n, i][:],
+                lhsT=w2_codes[k][:, P * i : P * (i + 1)].bitcast(FP8X4),
+                lhsT_scale=w2_scl[k][:, P * i : P * (i + 1)],
+                rhs=h_codes[k][n][:].bitcast(FP8X4),
+                rhs_scale=h_scl[k][n][:],
+                start=(k == 0),
+                stop=(k == NG - 1),
+            )
+
+        def finish(n, i):
+            o = op.tile([P, 512], F32, name="o%d_%d" % (n, i))
+            cols = slice(512 * n, 512 * (n + 1))
+            nc.vector.scalar_tensor_tensor(
+                out=o[:], in0=acc[n, i][:], scalar=gamma_sb[:, i, 0:1], in1=r_sb[:, i, cols], op0=MULT, op1=ADD
+            )
+            nc.sync.dma_start(out=out[P * i : P * (i + 1), cols], in_=o[:])
+
+        load_w1(0)
+        for q in range(4):
+            nc.scalar.dma_start(out=w1s[32 * q : 32 * (q + 1), :], in_=w1_scale[q].partition_broadcast(32))
+        for p in range(4):
+            load_y(p)
+        load_w1(1)
+        load_w2(0)
+        load_w2(1)
+        load_w1(2)
+        load_w2(2)
+        load_w2(3)
+        load_w1(3)
+        nc.gpsimd.dma_start(out=w2s_all[:], in_=w2_scale.partition_broadcast(P))
+        nc.gpsimd.dma_start(out=g_sb[:].rearrange("p (k t) -> p k t", t=4), in_=g.rearrange("(k p t) -> p k t", p=P, t=4))
+        make_identity(nc, ident[:])
+        for q in range(4):
+            nc.gpsimd.tensor_copy(
+                out=w2s[32 * q : 32 * (q + 1)],
+                in_=w2s_all[32 * q : 32 * (q + 1)].rearrange("p i (k q) -> p i k q", q=4)[:, :, :, q],
+            )
+        nc.sync.dma_start(out=r_sb[:], in_=r.rearrange("(i p) n -> p i n", p=P))
+        nc.gpsimd.dma_start(out=gamma_sb[:, :, 0:1], in_=gamma.rearrange("(i p) -> p i", p=P).unsqueeze(2))
+
+        widen("v", w1_wide[0], w1_raw[0], 0, 1024)
+        widen("s", w1_wide[0], w1_raw[0], 1024, 2048)
+        for jb in range(4):
+            interleave_w1(0, jb)
+        ty = [turn_y(p) for p in range(4)]
+        exit_y("s", 0, ty[0])
+        exit_y("s", 1, ty[1])
+        quant_y(0)
+        quant_w1(0)
+        quant_y(1)
+        z = {}
+        for u in range(3):
+            z[u] = z_unit(u)
+        widen("s", w1_wide[1], w1_raw[1], 0, 2048)
+        exit_y("s", 2, ty[2])
+        exit_y("s", 3, ty[3])
+        interleave_w1(1, 0)
+        interleave_w1(1, 1)
+        quant_y(2)
+        interleave_w1(1, 2)
+        quant_y(3)
+        interleave_w1(1, 3)
+
+        after = {u: [] for u in range(32)}
+
+        def put(u, fn, *args):
+            after[u].append((fn, args))
+
+        put(0, quant_w1, 1)
+        for k, u0, s0 in ((2, 4, 2), (3, 12, 10)):
+            put(s0, widen, "s", w1_wide[k], w1_raw[k], 0, 2048)
+            for jb in range(4):
+                put(u0 + jb, interleave_w1, k, jb)
+            put(u0 + 5, quant_w1, k)
+        for i, s0 in ((0, 4), (1, 6), (2, 8), (3, 12)):
+            put(s0, widen, "s", w2_wide[i], w2_raw[i], 0, 2048)
+        order = [(0, k) for k in range(4)] + [(1, k) for k in range(4)]
+        for s, (ip, k) in enumerate(order):
+            u = 7 + 2 * s
+            put(u, turn_w2, ip, k, s % 4)
+            put(u + 2, exit_w2, 2 * ip, k)
+            put(u + 2, exit_w2, 2 * ip + 1, k)
+            if ip == 1:
+                put(u + 3, quant_w2, k)
+        for k in range(3):
+            for i in range(4):
+                put(25 + k, stage2, 0, i, k)
+        for i in range(4):
+            put(28, stage2, 0, i, 3)
+        for i in range(3):
+            put(29 + i, finish, 0, i)
+            for k in range(3):
+                put(29 + i, stage2, 1, i, k)
+        for k in range(3):
+            put(31, stage2, 1, 3, k)
+
+        for u in range(32):
+            if u + 3 < 32:
+                z[u + 3] = z_unit(u + 3)
+            gelu(u, z[u])
+            gain(u)
+            if u % 2 == 0 and u:
+                quant_h(u // 2 - 1)
+            for fn, args in after[u]:
+                fn(*args)
+        quant_h(15)
+        finish(0, 3)
+        for i in range(4):
+            stage2(1, i, 3)
+        for i in range(4):
+            finish(1, i)

@@ -20,7 +20,7 @@ NG = H // 512
 NI = C // P
 FLOPS = 2 * NPOS * C * H * 2
 
-S_EXIT = [(1, k) for k in range(4)]
+PLAN = {'w1w': {1: ('v', -1), 2: ('v', 0), 3: ('s', 7)}, 'w1i': {1: (-1, -1, -1, -1), 2: (1, 2, 6, 8), 3: (9, 9, 9, 14)}, 'w2w': {0: ('s', 0), 1: ('v', 0), 2: ('v', -1), 3: ('s', 12)}, 'turn': (7, 7, 9, 12, 14, 15, 16, 16), 'ex': (('s', 2), ('s', 3), ('v', 1), ('s', 2), ('v', 0), ('s', 0), ('s', 2), ('s', 3)), 's2': (21, 26, 28), 'fin0': (29, 29, 30, 32), 's2b': 30, 'w10': 'vs'}
 
 
 def tile_convnext_pointwise_pair_d7_kernel(
@@ -161,12 +161,12 @@ def tile_convnext_pointwise_pair_d7_kernel(
                     nc.tensor.transpose(t[:, ii, u, :], words[:, 256 * k + u : 256 * (k + 1) : 2], ident[:])
             tb[ip, k] = t
 
-        def exit_w2(i, k):
+        def exit_w2(eng, i, k):
             o = w2_grp[k][:, 512 * i : 512 * (i + 1)].rearrange("p (r u e) -> p r u e", u=2, e=2)
             s = tb[i // 2, k][:, i % 2].rearrange("p u r -> p (u r)").bitcast(BF16)
             s = s.rearrange("p (u r e) -> p r u e", u=2, e=2)
             col = w2s[:, i, k : k + 1]
-            if (i // 2, k) in S_EXIT:
+            if eng == "s":
                 nc.scalar.activation(out=o, in_=s, func=COPY, scale=col)
             else:
                 nc.vector.tensor_scalar(out=o, in0=s, scalar1=col, scalar2=None, op0=MULT)
@@ -176,7 +176,7 @@ def tile_convnext_pointwise_pair_d7_kernel(
 
         def stage2(n, i, k):
             if k == 0:
-                acc[n, i] = psum.tile([P, 512], F32, name="z0" if (n, i) == (1, 3) else "a%d" % i)
+                acc[n, i] = psum.tile([P, 512], F32, name=("z%d" if n else "a%d") % i)
             nc.tensor.matmul_mx(
                 out=acc[n, i][:],
                 lhsT=w2_codes[k][:, P * i : P * (i + 1)].bitcast(FP8X4),
@@ -218,8 +218,8 @@ def tile_convnext_pointwise_pair_d7_kernel(
         nc.sync.dma_start(out=r_sb[:], in_=r.rearrange("(i p) n -> p i n", p=P))
         nc.gpsimd.dma_start(out=gamma_sb[:, :, 0:1], in_=gamma.rearrange("(i p) -> p i", p=P).unsqueeze(2))
 
-        widen("v", w1_wide[0], w1_raw[0], 0, 1024)
-        widen("s", w1_wide[0], w1_raw[0], 1024, 2048)
+        widen(PLAN["w10"][0], w1_wide[0], w1_raw[0], 0, 1024)
+        widen(PLAN["w10"][1], w1_wide[0], w1_raw[0], 1024, 2048)
         for jb in range(4):
             interleave_w1(0, jb)
         ty = [turn_y(p) for p in range(4)]
@@ -231,49 +231,48 @@ def tile_convnext_pointwise_pair_d7_kernel(
         z = {}
         for u in range(3):
             z[u] = z_unit(u)
-        widen("s", w1_wide[1], w1_raw[1], 0, 2048)
-        exit_y("s", 2, ty[2])
-        exit_y("s", 3, ty[3])
-        interleave_w1(1, 0)
-        interleave_w1(1, 1)
-        quant_y(2)
-        interleave_w1(1, 2)
-        quant_y(3)
-        interleave_w1(1, 3)
 
-        after = {u: [] for u in range(32)}
+        after = {u: [] for u in range(-1, 33)}
 
         def put(u, fn, *args):
             after[u].append((fn, args))
 
-        put(0, quant_w1, 1)
-        for k, u0, s0 in ((2, 4, 2), (3, 12, 10)):
-            put(s0, widen, "s", w1_wide[k], w1_raw[k], 0, 2048)
+        for k in (1, 2, 3):
+            e, s0 = PLAN["w1w"][k]
+            put(s0, widen, e, w1_wide[k], w1_raw[k], 0, 2048)
+        put(-1, exit_y, "s", 2, ty[2])
+        put(-1, exit_y, "s", 3, ty[3])
+        put(-1, quant_y, 2)
+        put(-1, quant_y, 3)
+        for k in (1, 2, 3):
             for jb in range(4):
-                put(u0 + jb, interleave_w1, k, jb)
-            put(u0 + 5, quant_w1, k)
-        for i, s0 in ((0, 4), (1, 6), (2, 8), (3, 12)):
-            put(s0, widen, "s", w2_wide[i], w2_raw[i], 0, 2048)
+                put(PLAN["w1i"][k][jb], interleave_w1, k, jb)
+            put(PLAN["w1i"][k][3] + 1, quant_w1, k)
+        for i in range(4):
+            e, s0 = PLAN["w2w"][i]
+            put(s0, widen, e, w2_wide[i], w2_raw[i], 0, 2048)
         order = [(0, k) for k in range(4)] + [(1, k) for k in range(4)]
         for s, (ip, k) in enumerate(order):
-            u = 7 + 2 * s
+            u = PLAN["turn"][s]
             put(u, turn_w2, ip, k, s % 4)
-            put(u + 2, exit_w2, 2 * ip, k)
-            put(u + 2, exit_w2, 2 * ip + 1, k)
+            e, lag = PLAN["ex"][s]
+            put(u + lag, exit_w2, e, 2 * ip, k)
+            put(u + lag, exit_w2, e, 2 * ip + 1, k)
             if ip == 1:
-                put(u + 3, quant_w2, k)
+                put(u + lag + 1, quant_w2, k)
         for k in range(3):
             for i in range(4):
-                put(25 + k, stage2, 0, i, k)
+                put(PLAN["s2"][k], stage2, 0, i, k)
         for i in range(4):
             put(28, stage2, 0, i, 3)
-        for i in range(3):
-            put(29 + i, finish, 0, i)
-            for k in range(3):
-                put(29 + i, stage2, 1, i, k)
+        for i in range(4):
+            put(PLAN["fin0"][i], finish, 0, i)
         for k in range(3):
-            put(31, stage2, 1, 3, k)
+            for i in range(4):
+                put(PLAN["s2b"] + k, stage2, 1, i, k)
 
+        for fn, args in after[-1]:
+            fn(*args)
         for u in range(32):
             if u + 3 < 32:
                 z[u + 3] = z_unit(u + 3)
@@ -284,7 +283,8 @@ def tile_convnext_pointwise_pair_d7_kernel(
             for fn, args in after[u]:
                 fn(*args)
         quant_h(15)
-        finish(0, 3)
+        for fn, args in after[32]:
+            fn(*args)
         for i in range(4):
             stage2(1, i, 3)
         for i in range(4):

from contextlib import ExitStack

import concourse.mybir as mybir
from concourse.masks import make_identity

F32 = mybir.dt.float32
BF16 = mybir.dt.bfloat16
U32 = mybir.dt.uint32
U8 = mybir.dt.uint8
FP8 = mybir.dt.float8_e4m3fn
FP8X4 = mybir.dt.float8_e4m3fn_x4
MULT = mybir.AluOpType.mult
ADD = mybir.AluOpType.add
GELU = mybir.ActivationFunctionType.Gelu_apprx_tanh
COPY = mybir.ActivationFunctionType.Copy

P = 128
NPOS, C, H = 1024, 512, 2048
NG = H // 512
NI = C // P
FLOPS = 2 * NPOS * C * H * 2

PLAN = {'w1w': {1: ('v', -1), 2: ('v', 0), 3: ('s', 7)}, 'w1i': {1: (-1, -1, -1, -1), 2: (1, 2, 6, 8), 3: (9, 9, 9, 14)}, 'w2w': {0: ('s', 0), 1: ('v', 0), 2: ('v', -1), 3: ('s', 12)}, 'turn': (7, 7, 9, 12, 14, 15, 16, 16), 'ex': (('s', 2), ('s', 3), ('v', 1), ('s', 2), ('v', 0), ('s', 0), ('s', 2), ('s', 3)), 's2': (21, 26, 28), 'fin0': (29, 29, 30, 32), 's2b': 30, 'w10': 'vs'}


def tile_convnext_pointwise_pair_d7_kernel(
    tc, y, w1_bytes, w1_scale, g, w2_bytes, w2_scale, gamma, r, out
):
    nc = tc.nc
    with ExitStack() as ctx:
        keep = ctx.enter_context(tc.tile_pool(name="keep", bufs=1))
        gelp = ctx.enter_context(tc.tile_pool(name="gelp", bufs=12))
        hp = ctx.enter_context(tc.tile_pool(name="hp", bufs=3))
        op = ctx.enter_context(tc.tile_pool(name="op", bufs=1))
        psum = ctx.enter_context(tc.psum_pool(name="psum", bufs=1))
        ctx.enter_context(tc.manual_schedule())

        def sb(shape, dt, name):
            return keep.tile(shape, dt, name=name, align_bytes=64)

        ident = sb([P, P], F32, "ident")
        w1s = sb([P, 16], F32, "w1s")
        w2s_all = sb([P, 4, 16], F32, "w2s_all")
        w2s = sb([P, 4, 4], F32, "w2s")
        g_sb = sb([P, 16], BF16, "g_sb")
        gamma_sb = sb([P, 4, 2], BF16, "gamma_sb")
        y_sb = [sb([P, 2, C], BF16, "y_sb%d" % p) for p in range(4)]
        y_grp = [sb([P, 1024], BF16, "y_grp%d" % p) for p in range(4)]
        y_codes = sb([P, NPOS], U32, "y_codes")
        y_scl = sb([P, NPOS], U8, "y_scl")
        w1_raw = [sb([P, 2048], U8, "w1_raw%d" % k) for k in range(NG)]
        w1_wide = [sb([P, 2048], BF16, "w1_wide%d" % k) for k in range(NG)]
        w1_grp = [sb([P, 2048], BF16, "w1_grp%d" % k) for k in range(NG)]
        w1_codes = [sb([P, 512], U32, "w1_codes%d" % k) for k in range(NG)]
        w1_scl = [sb([P, 512], U8, "w1_scl%d" % k) for k in range(NG)]
        w2_raw = [sb([P, 2048], U8, "w2_raw%d" % i) for i in range(NI)]
        w2_wide = [sb([P, 2048], BF16, "w2_wide%d" % i) for i in range(NI)]
        w2_grp = [sb([P, 2048], BF16, "w2_grp%d" % k) for k in range(NG)]
        w2_codes = [sb([P, 512], U32, "w2_codes%d" % k) for k in range(NG)]
        w2_scl = [sb([P, 512], U8, "w2_scl%d" % k) for k in range(NG)]
        h_codes = [[sb([P, 512], U32, "h_codes%d_%d" % (k, n)) for n in range(2)] for k in range(NG)]
        h_scl = [[sb([P, 512], U8, "h_scl%d_%d" % (k, n)) for n in range(2)] for k in range(NG)]
        r_sb = sb([P, NI, NPOS], BF16, "r_sb")

        gel = {}
        hbf = {}
        acc = {}
        tb = {}

        def load_w1(k):
            src = w1_bytes.rearrange("(p t) n -> p t n", t=4)[:, :, 512 * k : 512 * (k + 1)]
            nc.sync.dma_start(out=w1_raw[k][:].rearrange("p (t n) -> p t n", t=4), in_=src)

        def load_y(p):
            nc.sync.dma_start(
                out=y_sb[p][:], in_=y[256 * p : 256 * (p + 1), :].rearrange("(a p) k -> p a k", p=P)
            )

        def load_w2(i):
            nc.sync.dma_start(out=w2_raw[i][:], in_=w2_bytes[P * i : P * (i + 1), :])

        def widen(eng, dst, src, lo, hi):
            d, s = dst[:, lo:hi], src[:, lo:hi].bitcast(FP8)
            if eng == "s":
                nc.scalar.copy(out=d, in_=s)
            else:
                nc.vector.tensor_copy(out=d, in_=s)

        def interleave_w1(k, jb):
            o = w1_grp[k][:].rearrange("p (t m j) -> p m j t", t=4, j=4)[:, 32 * jb : 32 * (jb + 1)]
            i = w1_wide[k][:].rearrange("p (j m t) -> p m j t", j=4, t=4)[:, 32 * jb : 32 * (jb + 1)]
            nc.vector.tensor_scalar(
                out=o, in0=i, scalar1=w1s[:, 4 * k + jb : 4 * k + jb + 1], scalar2=None, op0=MULT
            )

        def quant_w1(k):
            nc.vector.quantize_mx(out=w1_codes[k][:].bitcast(FP8X4), scales=w1_scl[k][:], in_=w1_grp[k][:])

        def turn_y(p):
            t = psum.tile([P, 2, 2, P], F32, name="a%d" % p)
            words = y_sb[p][:].rearrange("p a k -> p (a k)").bitcast(F32)
            for a in range(2):
                for u in range(2):
                    nc.tensor.transpose(t[:, a, u, :], words[:, 256 * a + u : 256 * (a + 1) : 2], ident[:])
            return t

        def exit_y(eng, p, t):
            o = y_grp[p][:].bitcast(F32).rearrange("p (a r u) -> p a r u", a=2, u=2)
            i = t[:].rearrange("p a u r -> p a r u")
            if eng == "s":
                nc.scalar.copy(out=o, in_=i)
            else:
                nc.vector.tensor_copy(out=o, in_=i)

        def quant_y(p):
            cols = slice(256 * p, 256 * (p + 1))
            nc.vector.quantize_mx(out=y_codes[:, cols].bitcast(FP8X4), scales=y_scl[:, cols], in_=y_grp[p][:])

        def z_unit(u):
            k, b = divmod(u, 8)
            z = psum.tile([P, 4, P], F32, name="z%d" % (u % 4))
            for t in range(4):
                nc.tensor.matmul_mx(
                    out=z[:, t, :],
                    lhsT=w1_codes[k][:, P * t : P * (t + 1)].bitcast(FP8X4),
                    lhsT_scale=w1_scl[k][:, P * t : P * (t + 1)],
                    rhs=y_codes[:, P * b : P * (b + 1)].bitcast(FP8X4),
                    rhs_scale=y_scl[:, P * b : P * (b + 1)],
                    start=True,
                    stop=True,
                )
            return z

        def gelu(u, z):
            a = gelp.tile([P, P, 4], F32, name="gel")
            nc.scalar.activation(out=a[:], in_=z[:].rearrange("p t n -> p n t"), func=GELU)
            gel[u] = a

        def gain(u):
            k = u // 8
            if u % 2 == 0:
                hb = hp.tile([P, 1024], BF16, name="hbf", align_bytes=64)
                hbf[u // 2] = hb
            o = hbf[u // 2][:, 512 * (u % 2) : 512 * (u % 2 + 1)].rearrange("p (n t) -> p n t", t=4)
            gk = g_sb[:, 4 * k : 4 * (k + 1)].unsqueeze(1).to_broadcast([P, P, 4])
            nc.vector.tensor_tensor(out=o, in0=gel[u][:], in1=gk, op=MULT)

        def quant_h(pair):
            k, q = divmod(pair, 4)
            n, c = divmod(q, 2)
            cols = slice(256 * c, 256 * (c + 1))
            nc.vector.quantize_mx(
                out=h_codes[k][n][:, cols].bitcast(FP8X4), scales=h_scl[k][n][:, cols], in_=hbf[pair][:]
            )

        def turn_w2(ip, k, bank):
            t = psum.tile([P, 2, 2, P], F32, name="a%d" % bank)
            for ii in range(2):
                words = w2_wide[2 * ip + ii][:].bitcast(F32)
                for u in range(2):
                    nc.tensor.transpose(t[:, ii, u, :], words[:, 256 * k + u : 256 * (k + 1) : 2], ident[:])
            tb[ip, k] = t

        def exit_w2(eng, i, k):
            o = w2_grp[k][:, 512 * i : 512 * (i + 1)].rearrange("p (r u e) -> p r u e", u=2, e=2)
            s = tb[i // 2, k][:, i % 2].rearrange("p u r -> p (u r)").bitcast(BF16)
            s = s.rearrange("p (u r e) -> p r u e", u=2, e=2)
            col = w2s[:, i, k : k + 1]
            if eng == "s":
                nc.scalar.activation(out=o, in_=s, func=COPY, scale=col)
            else:
                nc.vector.tensor_scalar(out=o, in0=s, scalar1=col, scalar2=None, op0=MULT)

        def quant_w2(k):
            nc.vector.quantize_mx(out=w2_codes[k][:].bitcast(FP8X4), scales=w2_scl[k][:], in_=w2_grp[k][:])

        def stage2(n, i, k):
            if k == 0:
                acc[n, i] = psum.tile([P, 512], F32, name=("z%d" if n else "a%d") % i)
            nc.tensor.matmul_mx(
                out=acc[n, i][:],
                lhsT=w2_codes[k][:, P * i : P * (i + 1)].bitcast(FP8X4),
                lhsT_scale=w2_scl[k][:, P * i : P * (i + 1)],
                rhs=h_codes[k][n][:].bitcast(FP8X4),
                rhs_scale=h_scl[k][n][:],
                start=(k == 0),
                stop=(k == NG - 1),
            )

        def finish(n, i):
            o = op.tile([P, 512], F32, name="o%d_%d" % (n, i))
            cols = slice(512 * n, 512 * (n + 1))
            nc.vector.scalar_tensor_tensor(
                out=o[:], in0=acc[n, i][:], scalar=gamma_sb[:, i, 0:1], in1=r_sb[:, i, cols], op0=MULT, op1=ADD
            )
            nc.sync.dma_start(out=out[P * i : P * (i + 1), cols], in_=o[:])

        load_w1(0)
        for q in range(4):
            nc.scalar.dma_start(out=w1s[32 * q : 32 * (q + 1), :], in_=w1_scale[q].partition_broadcast(32))
        for p in range(4):
            load_y(p)
        load_w1(1)
        load_w2(0)
        load_w2(1)
        load_w1(2)
        load_w2(2)
        load_w2(3)
        load_w1(3)
        nc.gpsimd.dma_start(out=w2s_all[:], in_=w2_scale.partition_broadcast(P))
        nc.gpsimd.dma_start(out=g_sb[:].rearrange("p (k t) -> p k t", t=4), in_=g.rearrange("(k p t) -> p k t", p=P, t=4))
        make_identity(nc, ident[:])
        for q in range(4):
            nc.gpsimd.tensor_copy(
                out=w2s[32 * q : 32 * (q + 1)],
                in_=w2s_all[32 * q : 32 * (q + 1)].rearrange("p i (k q) -> p i k q", q=4)[:, :, :, q],
            )
        nc.sync.dma_start(out=r_sb[:], in_=r.rearrange("(i p) n -> p i n", p=P))
        nc.gpsimd.dma_start(out=gamma_sb[:, :, 0:1], in_=gamma.rearrange("(i p) -> p i", p=P).unsqueeze(2))

        widen(PLAN["w10"][0], w1_wide[0], w1_raw[0], 0, 1024)
        widen(PLAN["w10"][1], w1_wide[0], w1_raw[0], 1024, 2048)
        for jb in range(4):
            interleave_w1(0, jb)
        ty = [turn_y(p) for p in range(4)]
        exit_y("s", 0, ty[0])
        exit_y("s", 1, ty[1])
        quant_y(0)
        quant_w1(0)
        quant_y(1)
        z = {}
        for u in range(3):
            z[u] = z_unit(u)

        after = {u: [] for u in range(-1, 33)}

        def put(u, fn, *args):
            after[u].append((fn, args))

        for k in (1, 2, 3):
            e, s0 = PLAN["w1w"][k]
            put(s0, widen, e, w1_wide[k], w1_raw[k], 0, 2048)
        put(-1, exit_y, "s", 2, ty[2])
        put(-1, exit_y, "s", 3, ty[3])
        put(-1, quant_y, 2)
        put(-1, quant_y, 3)
        for k in (1, 2, 3):
            for jb in range(4):
                put(PLAN["w1i"][k][jb], interleave_w1, k, jb)
            put(PLAN["w1i"][k][3] + 1, quant_w1, k)
        for i in range(4):
            e, s0 = PLAN["w2w"][i]
            put(s0, widen, e, w2_wide[i], w2_raw[i], 0, 2048)
        order = [(0, k) for k in range(4)] + [(1, k) for k in range(4)]
        for s, (ip, k) in enumerate(order):
            u = PLAN["turn"][s]
            put(u, turn_w2, ip, k, s % 4)
            e, lag = PLAN["ex"][s]
            put(u + lag, exit_w2, e, 2 * ip, k)
            put(u + lag, exit_w2, e, 2 * ip + 1, k)
            if ip == 1:
                put(u + lag + 1, quant_w2, k)
        for k in range(3):
            for i in range(4):
                put(PLAN["s2"][k], stage2, 0, i, k)
        for i in range(4):
            put(28, stage2, 0, i, 3)
        for i in range(4):
            put(PLAN["fin0"][i], finish, 0, i)
        for k in range(3):
            for i in range(4):
                put(PLAN["s2b"] + k, stage2, 1, i, k)

        for fn, args in after[-1]:
            fn(*args)
        for u in range(32):
            if u + 3 < 32:
                z[u + 3] = z_unit(u + 3)
            gelu(u, z[u])
            gain(u)
            if u % 2 == 0 and u:
                quant_h(u // 2 - 1)
            for fn, args in after[u]:
                fn(*args)
        quant_h(15)
        for fn, args in after[32]:
            fn(*args)
        for i in range(4):
            stage2(1, i, 3)
        for i in range(4):
            finish(1, i)
